import numpy as np
import ml_dtypes


def mxq(x, axis, fmt="e4m3"):
    dtype, down = {"e4m3": (ml_dtypes.float8_e4m3fn, 7), "e5m2": (ml_dtypes.float8_e5m2, 14)}[fmt]
    v = np.moveaxis(np.asarray(x, np.float32).astype(ml_dtypes.bfloat16).astype(np.float64), axis, -1)
    blocks = v.reshape(v.shape[:-1] + (-1, 32))
    amax = np.abs(blocks).max(-1, keepdims=True)
    byte = np.maximum(np.where(amax > 0, np.frexp(amax)[1] - 1 + 127, 0) - down, 1)
    scale = np.exp2(byte - 127.0)
    codes = (blocks / scale).astype(np.float32).astype(dtype).astype(np.float64)
    return np.moveaxis((codes * scale).reshape(v.shape), -1, axis)


WIDE = False


def mx_kscale(k):
    if not WIDE:
        return np.ones(k)
    levels = np.array([10, -10, 5, -5, 0])
    if k % 512:
        return np.exp2(np.random.permutation(np.resize(levels, k // 32))).repeat(32)
    a = np.empty((k // 512, 16))
    for p in range(k // 512):
        a[p, :8] = np.random.permutation(np.resize(levels, 8))
        for g in range(8):
            far = levels[np.abs(levels - a[p, g]) >= 10]
            a[p, g + 8] = far[np.random.randint(len(far))]
    return np.exp2(a.ravel()).repeat(32)


BF16 = ml_dtypes.bfloat16


def bf(x):
    return np.asarray(x, np.float32).astype(BF16)


def f64(x):
    return np.asarray(x).astype(np.float64)


D, J, KO, KI, Q = 1024, 2048, 512, 1024, 512

SPREAD_W, SPREAD_D, SPREAD_SIZE = 1.5, 1.0, 0.4


def setup_inputs():
    s = mx_kscale(KO)
    r = mx_kscale(KI)
    t = mx_kscale(D)
    mean = np.exp((SPREAD_W ** 2 + SPREAD_D ** 2) / 2)
    size = np.exp(SPREAD_SIZE * np.random.standard_normal(J))
    u = np.exp(SPREAD_W * np.random.standard_normal((D, KO))) / (KO * mean)
    v = np.exp(SPREAD_W * np.random.standard_normal((D, KI))) / (KI * mean)
    y = np.exp(SPREAD_D * np.random.standard_normal((KO, J))) * size
    x = np.exp(SPREAD_D * np.random.standard_normal((KI, J))) * size
    return {"u": bf(u * s * t[:, None]),
            "y": bf(y / s[:, None]),
            "u0": bf(0.4 * np.random.standard_normal(D) * t),
            "v": bf(v * r),
            "x": bf(x / r[:, None]),
            "a": bf(np.random.standard_normal((Q, D)) / np.sqrt(D) / t)}


def reference(u, y, u0, v, x, a):
    num = mxq(f64(u), 1, "e4m3") @ mxq(f64(y), 0, "e4m3")
    den = mxq(f64(v), 1, "e4m3") @ mxq(f64(x), 0, "e4m3")
    e = (num + f64(u0)[:, None]) / den
    return mxq(f64(a), 1, "e4m3") @ mxq(e, 0, "e4m3")

@@ -1,0 +1,318 @@
+from contextlib import ExitStack
+
+import concourse.mybir as mybir
+from concourse.masks import make_identity
+
+D, J, KO, KI, Q = 1024, 2048, 512, 1024, 512
+FLOPS = 2 * J * (D * KO + D * KI + Q * D)
+
+F32 = mybir.dt.float32
+BF16 = mybir.dt.bfloat16
+U32 = mybir.dt.uint32
+U8 = mybir.dt.uint8
+FP8X4 = mybir.dt.float8_e4m3fn_x4
+ACT = mybir.ActivationFunctionType
+ALU = mybir.AluOpType
+
+P = 128
+PACK = 4
+K_PASS = P * PACK
+BANK = 512
+PANEL = 512
+CHUNKS = (512,512,512,256,256)
+S_SHARE_HEAD = [128,256,0]
+S_SHARE = [[0,0,0],[128,128,128],[128,128,128]]
+XSLOTS = [[1,3,5],[8,10,13],[16,18,21]]
+NUM_LAG = 3
+STT_LAG = 3
+V_OUTS = [14]
+RECIP_BUFS = 6
+A_SLOT = 6
+OUT_LAG = 3
+OUT_STEP = 1
+OUT_EVAC_LAG = 1
+V_SLOTS = [-8,0,-1,0,1,2,3,4]
+V_LAG = 0
+U_SLOTS = [0,0,3,3]
+U_LAG = 0
+U_ON_V = [False, False, False, False]
+Y_SLOT = -1
+E_LAG = 1
+DEN_BUFS = 2
+NUM_BUFS = 3
+AUX_BUFS = 3
+
+
+def tile_dea_cross_efficiency_s7_kernel(tc, u, y, u0, v, x, a, out):
+    nc = tc.nc
+    groups = D // K_PASS
+    panels = J // PANEL
+
+    with ExitStack() as ctx:
+        keep = ctx.enter_context(tc.tile_pool(name="keep", bufs=1))
+        work = ctx.enter_context(tc.tile_pool(name="work", bufs=3))
+        psum = ctx.enter_context(tc.psum_pool(name="psum", bufs=1))
+        ctx.enter_context(tc.manual_schedule())
+
+        v_rows = v.rearrange("(g m t) k -> g m t k", g=groups, t=PACK)
+        u_rows = u.rearrange("(g m t) k -> g m t k", g=groups, t=PACK)
+        a_rows = a.rearrange("(m s) d -> m s d", s=PACK)
+        out_rows = out.rearrange("(m s) j -> m s j", s=PACK)
+        data_rows = [x[0:K_PASS, :], x[K_PASS : 2 * K_PASS, :], y]
+
+        data_raw, weight_raw = {}, {}
+
+        def load_data(panel, c, count):
+            raw = keep.tile([P, PACK, count * PANEL], BF16, name="data_raw_%d_%d" % (panel, c))
+            cols = slice(panel * PANEL, (panel + count) * PANEL)
+            nc.sync.dma_start(out=raw[:], in_=data_rows[c][:, cols].rearrange("(p t) n -> p t n", t=PACK))
+            for n in range(count):
+                data_raw[panel + n, c] = raw[:, :, n * PANEL : (n + 1) * PANEL]
+
+        def load_weight(name, rows, banks):
+            raw = keep.tile([P, len(banks) * 2 * K_PASS], BF16, name="raw_%s_%d" % (name, banks[0]))
+            nc.sync.dma_start(out=raw[:].rearrange("p (t k) -> p t k", t=rows.shape[1]), in_=rows)
+            words = raw[:].bitcast(F32)
+            for n, bank in enumerate(banks):
+                weight_raw[name, bank] = words[:, n * BANK : (n + 1) * BANK]
+
+        bias = keep.tile([P, groups, PACK], BF16, name="bias")
+        nc.scalar.dma_start(out=bias[:], in_=u0.rearrange("(g p t) -> p g t", g=groups, t=PACK))
+
+        load_weight("v", v_rows[0][:, 0:1, :], [0])
+        load_data(0, 0, 1)
+        load_data(0, 1, 1)
+        load_weight("v", v_rows[0][:, 1:2, :], [1])
+        load_weight("v", v_rows[0][:, 2:4, :], [2, 3])
+        load_data(0, 2, 1)
+        load_weight("u", u_rows[0], [0, 1])
+        load_weight("v", v_rows[1][:, 0:2, :], [4, 5])
+        load_data(1, 0, 1)
+        load_weight("v", v_rows[1][:, 2:4, :], [6, 7])
+        load_weight("u", u_rows[1], [2, 3])
+        load_data(1, 1, 1)
+        load_data(1, 2, 1)
+        load_weight("a", a_rows, [0, 1, 2, 3])
+        for c in range(3):
+            load_data(2, c, 2)
+
+        ident = keep.tile([P, P], F32, name="ident")
+        make_identity(nc, ident[:])
+        warm = keep.tile([P, 1], F32, name="warm")
+        nc.scalar.activation(out=warm[:], in_=ident[:, 0:1], func=ACT.Abs_reciprocal_sqrt, bias=1.0)
+
+        codes, scales, staged, banks = {}, {}, {}, {}
+
+        def aux_bank():
+            return psum.tile([P, BANK], F32, name="aux", bufs=AUX_BUFS)
+
+        def quantize(key, width):
+            name = "_".join(str(part) for part in key)
+            code = keep.tile([P, width], U32, name="codes_" + name, align_bytes=64)
+            scale = keep.tile([P, width], U8, name="scales_" + name, align_bytes=64)
+            nc.vector.quantize_mx(out=code[:].bitcast(FP8X4), scales=scale[:], in_=staged[key][:, 0 : PACK * width])
+            codes[key], scales[key] = code, scale
+
+        def interleave(copy, dst, src, lo, hi):
+            copy(
+                out=dst[:, PACK * lo : PACK * hi].rearrange("p (c i t) -> p c t i", i=4, t=PACK),
+                in_=src[:, :, lo:hi].rearrange("p t (c i) -> p c t i", i=4),
+            )
+
+        def turn_weight(name, b):
+            bank = aux_bank()
+            words = weight_raw[name, b]
+            for half in range(2):
+                for w in range(2):
+                    col = (2 * half + w) * P
+                    nc.tensor.transpose(
+                        bank[:, col : col + P], words[:, 256 * half + w : 256 * (half + 1) : 2], ident[:]
+                    )
+            banks[name, b] = bank
+
+        def empty_weight(name, b, copy):
+            dst = work.tile([P, 2 * K_PASS], BF16, name="weight_staged", align_bytes=64)
+            copy(
+                out=dst[:].bitcast(F32).rearrange("p (h m w) -> p h m w", h=2, w=2),
+                in_=banks[name, b][:].rearrange("p (h w m) -> p h m w", h=2, w=2),
+            )
+            staged[name, b] = dst
+
+        def stage_data(panel, c, share):
+            dst = work.tile([P, PACK * PANEL], BF16, name="data_staged", align_bytes=64)
+            staged["data", panel, c] = dst
+            interleave(nc.vector.tensor_copy, dst, data_raw[panel, c], share, PANEL)
+
+        def stage_data_scalar(panel, c, share):
+            if share:
+                interleave(nc.scalar.copy, staged["data", panel, c], data_raw[panel, c], 0, share)
+
+        def mx(acc, left, left_col, right, right_col, width, start, stop):
+            lcols = slice(left_col, left_col + P)
+            rcols = slice(right_col, right_col + width)
+            nc.tensor.matmul_mx(
+                out=acc,
+                lhsT=codes[left][:, lcols].bitcast(FP8X4),
+                lhsT_scale=scales[left][:, lcols],
+                rhs=codes[right][:, rcols].bitcast(FP8X4),
+                rhs_scale=scales[right][:, rcols],
+                start=start,
+                stop=stop,
+            )
+
+        starts = [sum(CHUNKS[:n]) for n in range(len(CHUNKS))]
+        steps = []
+        for ch, width in enumerate(CHUNKS):
+            for g in range(groups):
+                for t0 in range(0, PACK, BANK // width):
+                    steps.append((ch, g, t0))
+        roots, recips, ratio = {}, {}, {}
+
+        def den_matmul(i):
+            ch, g, t0 = steps[i]
+            width = CHUNKS[ch]
+            panel, col = divmod(starts[ch], PANEL)
+            bank = psum.tile([P, BANK], F32, name="den", bufs=DEN_BUFS)
+            for n in range(BANK // width):
+                for c in range(2):
+                    mx(bank[:, n * width : (n + 1) * width], ("v", PACK * g + t0 + n), c * P,
+                       ("data", panel, c), col, width, c == 0, c == 1)
+            banks["den", i] = bank
+
+        def num_matmul(i):
+            ch, g, t0 = steps[i]
+            width = CHUNKS[ch]
+            panel, col = divmod(starts[ch], PANEL)
+            bank = psum.tile([P, BANK], F32, name="num", bufs=NUM_BUFS)
+            for n in range(BANK // width):
+                pair, half = divmod(PACK * g + t0 + n, 2)
+                mx(bank[:, n * width : (n + 1) * width], ("u", pair), half * P,
+                   ("data", panel, 2), col, width, True, True)
+            banks["num", i] = bank
+
+        def root(i):
+            r = work.tile([P, BANK], F32, name="root")
+            nc.scalar.activation(out=r[:], in_=banks["den", i][:], func=ACT.Abs_reciprocal_sqrt)
+            roots[i] = r
+
+        def square(i):
+            r2 = work.tile([P, BANK], F32, name="recip", bufs=RECIP_BUFS)
+            nc.scalar.activation(out=r2[:], in_=roots[i][:], func=ACT.Square)
+            recips[i] = r2
+
+        def divide(i):
+            ch, g, t0 = steps[i]
+            width = CHUNKS[ch]
+            if t0 == 0:
+                rows = work.tile([P, PACK * PANEL], BF16, name="ratio_rows", bufs=2)
+                ratio[ch, g] = rows[:, 0 : PACK * width].rearrange("p (t n) -> p t n", t=PACK)
+            for n in range(BANK // width):
+                cols = slice(n * width, (n + 1) * width)
+                nc.vector.scalar_tensor_tensor(
+                    out=ratio[ch, g][:, t0 + n, :], in0=banks["num", i][:, cols],
+                    scalar=bias[:, g, t0 + n : t0 + n + 1], in1=recips[i][:, cols],
+                    op0=ALU.add, op1=ALU.mult,
+                )
+
+        def stage_ratio(ch, g):
+            dst = work.tile([P, PACK * PANEL], BF16, name="ratio_staged", bufs=2, align_bytes=64)
+            staged["e", ch, g] = dst
+            interleave(nc.vector.tensor_copy, dst, ratio[ch, g], 0, CHUNKS[ch])
+
+        def out_matmul(ch, s0):
+            width = CHUNKS[ch]
+            bank = aux_bank()
+            for n in range(BANK // width):
+                for g in range(groups):
+                    mx(bank[:, n * width : (n + 1) * width], ("a", s0 + n), g * P,
+                       ("e", ch, g), 0, width, g == 0, g == groups - 1)
+            banks["out", ch, s0] = bank
+
+        def store(ch, s0, copy):
+            width = CHUNKS[ch]
+            count = BANK // width
+            res = work.tile([P, BANK], F32, name="result", bufs=6)
+            copy(out=res[:], in_=banks["out", ch, s0][:])
+            nc.sync.dma_start(
+                out=out_rows[:, s0 : s0 + count, starts[ch] : starts[ch] + width],
+                in_=res[:].rearrange("p (s n) -> p s n", s=count),
+            )
+
+        last = len(steps)
+        slots = range(-4, last + 12)
+        early_v = {i: [] for i in slots}
+        first_v = {i: [] for i in slots}
+        late_v = {i: [] for i in slots}
+        pe = {i: [] for i in slots}
+        sc = {i: [] for i in slots}
+
+        def plan_weight(name, b, slot, lag, on_vector=False):
+            pe[slot].append(lambda: turn_weight(name, b))
+            if on_vector:
+                late_v[slot + 1].append(lambda: empty_weight(name, b, nc.vector.tensor_copy))
+                first_v[slot + 2].append(lambda: quantize((name, b), 2 * P))
+            else:
+                sc[slot + lag].append(lambda: empty_weight(name, b, nc.scalar.copy))
+                early_v[slot + lag + 1].append(lambda: quantize((name, b), 2 * P))
+
+        def plan_data(panel, c, slot, share):
+            late_v[slot].append(lambda: stage_data(panel, c, share))
+            sc[slot].append(lambda: stage_data_scalar(panel, c, share))
+            first_v[slot + 1].append(lambda: quantize(("data", panel, c), PANEL))
+
+        def plan_ratio(ch, g, slot):
+            late_v[slot].append(lambda: stage_ratio(ch, g))
+            first_v[slot + 1].append(lambda: quantize(("e", ch, g), CHUNKS[ch]))
+
+        def plan_out(ch, s0, slot, on_vector):
+            pe[slot].append(lambda: out_matmul(ch, s0))
+            if on_vector:
+                late_v[slot + 1].append(lambda: store(ch, s0, nc.vector.tensor_copy))
+            else:
+                sc[slot + OUT_EVAC_LAG].append(lambda: store(ch, s0, nc.scalar.copy))
+
+        plan_weight("v", 0, -4, 0)
+        plan_data(0, 0, -4, S_SHARE_HEAD[0])
+        plan_data(0, 1, -3, S_SHARE_HEAD[1])
+        plan_weight("v", 1, -2, 0)
+        plan_data(0, 2, Y_SLOT, S_SHARE_HEAD[2])
+        for b in range(2, 8):
+            plan_weight("v", b, V_SLOTS[b], V_LAG)
+        for b in range(4):
+            plan_weight("u", b, U_SLOTS[b], U_LAG, U_ON_V[b])
+        for b in range(4):
+            plan_weight("a", b, A_SLOT + b, 1)
+        for panel in range(1, panels):
+            for c in range(3):
+                plan_data(panel, c, XSLOTS[panel - 1][c], S_SHARE[panel - 1][c])
+        nout = 0
+        for i, (ch, g, t0) in enumerate(steps):
+            if t0 + BANK // CHUNKS[ch] == PACK:
+                plan_ratio(ch, g, i + STT_LAG + E_LAG)
+                if g == groups - 1:
+                    for n, s0 in enumerate(range(0, PACK, BANK // CHUNKS[ch])):
+                        tail = ch == len(CHUNKS) - 1
+                        plan_out(ch, s0, i + STT_LAG + E_LAG + OUT_LAG + (0 if tail else n * OUT_STEP), nout in V_OUTS)
+                        nout = nout + 1
+
+        for i in slots:
+            for job in early_v[i]:
+                job()
+            if 0 <= i - STT_LAG < last:
+                divide(i - STT_LAG)
+            for job in first_v[i]:
+                job()
+            for job in late_v[i]:
+                job()
+            if 0 <= i + 1 < last:
+                den_matmul(i + 1)
+            if 0 <= i + 1 - NUM_LAG < last:
+                num_matmul(i + 1 - NUM_LAG)
+            for job in pe[i]:
+                job()
+            if 0 <= i < last:
+                root(i)
+            if 0 <= i - 1 < last:
+                square(i - 1)
+            for job in sc[i]:
+                job()

@@ -20,27 +20,40 @@ K_PASS = P * PACK
 BANK = 512
 PANEL = 512
 CHUNKS = (512,512,512,256,256)
-S_SHARE_HEAD = [128,256,0]
-S_SHARE = [[0,0,0],[128,128,128],[128,128,128]]
-XSLOTS = [[1,3,5],[8,10,13],[16,18,21]]
-NUM_LAG = 3
+S_SHARE_HEAD = [128, 256, 0]
+OWN = [[1,0,1,64],[1,1,3,64],[1,2,5,64],[2,1,10,64],[3,1,18,64]]
+POOL_TILES = [(2,0),(2,2),(3,0),(3,2)]
+WINDOW_LAG = 2
+LOADS = [("v",0,1),("d",0,0,1),("d",0,1,1),("v",1,1),("d",0,2,1),("v",2,2),("u",0,2),("d",1,0,1),("v",4,2),("u",2,2),("v",6,2),("d",1,1,1),("d",1,2,1),("d",2,0,2),("d",2,1,2),("d",2,2,2),("a",0,4)]
+V_ON_V = [False,True]*4
+A_ON_V = [False]*4
+WARM = 0
+TAIL_SHARE = 0
+G_FIRST = 1
+Q_LAG = 3
+G_COLS = 416
+NUM_W = [3,3,4,4]
+OUT_LAG_W = 6
+W_FROM = 4
+TABLE_WARM = 0
+STT_LAG0 = 2
 STT_LAG = 3
-V_OUTS = [14]
+V_OUTS = []
 RECIP_BUFS = 6
-A_SLOT = 6
-OUT_LAG = 3
+A_SLOT = 11
+OUT_LAG = 2
 OUT_STEP = 1
 OUT_EVAC_LAG = 1
-V_SLOTS = [-8,0,-1,0,1,2,3,4]
-V_LAG = 0
-U_SLOTS = [0,0,3,3]
-U_LAG = 0
-U_ON_V = [False, False, False, False]
+V_SLOTS = [0,0,-1,-1,1,1,3,3]
+V_LAG = 1
+U_SLOTS = [-1,0,2,4]
+U_LAG = 1
+U_ON_V = [False]*4
 Y_SLOT = -1
 E_LAG = 1
 DEN_BUFS = 2
-NUM_BUFS = 3
-AUX_BUFS = 3
+NUM_BUFS = 4
+AUX_BUFS = 2
 
 
 def tile_dea_cross_efficiency_s7_kernel(tc, u, y, u0, v, x, a, out):
@@ -79,27 +92,23 @@ def tile_dea_cross_efficiency_s7_kernel(tc, u, y, u0, v, x, a, out):
         bias = keep.tile([P, groups, PACK], BF16, name="bias")
         nc.scalar.dma_start(out=bias[:], in_=u0.rearrange("(g p t) -> p g t", g=groups, t=PACK))
 
-        load_weight("v", v_rows[0][:, 0:1, :], [0])
-        load_data(0, 0, 1)
-        load_data(0, 1, 1)
-        load_weight("v", v_rows[0][:, 1:2, :], [1])
-        load_weight("v", v_rows[0][:, 2:4, :], [2, 3])
-        load_data(0, 2, 1)
-        load_weight("u", u_rows[0], [0, 1])
-        load_weight("v", v_rows[1][:, 0:2, :], [4, 5])
-        load_data(1, 0, 1)
-        load_weight("v", v_rows[1][:, 2:4, :], [6, 7])
-        load_weight("u", u_rows[1], [2, 3])
-        load_data(1, 1, 1)
-        load_data(1, 2, 1)
-        load_weight("a", a_rows, [0, 1, 2, 3])
-        for c in range(3):
-            load_data(2, c, 2)
+        for item in LOADS:
+            if item[0] == "v":
+                g, t0 = divmod(item[1], PACK)
+                load_weight("v", v_rows[g][:, t0 : t0 + item[2], :], list(range(item[1], item[1] + item[2])))
+            elif item[0] == "u":
+                g, t0 = divmod(2 * item[1], PACK)
+                load_weight("u", u_rows[g][:, t0 : t0 + 2 * item[2], :], list(range(item[1], item[1] + item[2])))
+            elif item[0] == "a":
+                load_weight("a", a_rows[:, item[1] : item[1] + item[2], :], list(range(item[1], item[1] + item[2])))
+            else:
+                load_data(item[1], item[2], item[3])
 
         ident = keep.tile([P, P], F32, name="ident")
         make_identity(nc, ident[:])
-        warm = keep.tile([P, 1], F32, name="warm")
-        nc.scalar.activation(out=warm[:], in_=ident[:, 0:1], func=ACT.Abs_reciprocal_sqrt, bias=1.0)
+        if TABLE_WARM:
+            warm = keep.tile([P, 1], F32, name="warm")
+            nc.scalar.activation(out=warm[:], in_=ident[:, 0:1], func=ACT.Abs_reciprocal_sqrt, bias=1.0)
 
         codes, scales, staged, banks = {}, {}, {}, {}
 
@@ -120,7 +129,7 @@ def tile_dea_cross_efficiency_s7_kernel(tc, u, y, u0, v, x, a, out):
             )
 
         def turn_weight(name, b):
-            bank = aux_bank()
+            bank = aux_bank() if name != "u" else psum.tile([P, BANK], F32, name="num", bufs=NUM_BUFS)
             words = weight_raw[name, b]
             for half in range(2):
                 for w in range(2):
@@ -139,9 +148,21 @@ def tile_dea_cross_efficiency_s7_kernel(tc, u, y, u0, v, x, a, out):
             staged[name, b] = dst
 
         def stage_data(panel, c, share):
-            dst = work.tile([P, PACK * PANEL], BF16, name="data_staged", align_bytes=64)
+            if (panel, c) == (1, 2) and POOL_TILES:
+                dst = work.tile([P, PACK * PANEL], BF16, name="pool_staged", bufs=1, align_bytes=64)
+            else:
+                dst = work.tile([P, PACK * PANEL], BF16, name="data_staged", align_bytes=64)
             staged["data", panel, c] = dst
             interleave(nc.vector.tensor_copy, dst, data_raw[panel, c], share, PANEL)
+
+        def stage_data_gpsimd(panel, c):
+            dst = work.tile([P, PACK * PANEL], BF16, name="pool_staged", bufs=1, align_bytes=64)
+            staged["data", panel, c] = dst
+            nc.gpsimd.tensor_scalar(
+                out=dst[:, 0 : PACK * G_COLS].rearrange("p (n t) -> p n t", t=PACK),
+                in0=data_raw[panel, c][:, :, 0:G_COLS].rearrange("p t n -> p n t"),
+                scalar1=1.0, scalar2=0.0, op0=ALU.mult, op1=ALU.add,
+            )
 
         def stage_data_scalar(panel, c, share):
             if share:
@@ -217,7 +238,10 @@ def tile_dea_cross_efficiency_s7_kernel(tc, u, y, u0, v, x, a, out):
         def stage_ratio(ch, g):
             dst = work.tile([P, PACK * PANEL], BF16, name="ratio_staged", bufs=2, align_bytes=64)
             staged["e", ch, g] = dst
-            interleave(nc.vector.tensor_copy, dst, ratio[ch, g], 0, CHUNKS[ch])
+            share = TAIL_SHARE if (ch, g) == (len(CHUNKS) - 1, groups - 1) else 0
+            if share:
+                interleave(nc.scalar.copy, dst, ratio[ch, g], 0, share)
+            interleave(nc.vector.tensor_copy, dst, ratio[ch, g], share, CHUNKS[ch])
 
         def out_matmul(ch, s0):
             width = CHUNKS[ch]
@@ -231,18 +255,40 @@ def tile_dea_cross_efficiency_s7_kernel(tc, u, y, u0, v, x, a, out):
         def store(ch, s0, copy):
             width = CHUNKS[ch]
             count = BANK // width
-            res = work.tile([P, BANK], F32, name="result", bufs=6)
+            res = work.tile([P, BANK], F32, name="result", bufs=8)
             copy(out=res[:], in_=banks["out", ch, s0][:])
             nc.sync.dma_start(
                 out=out_rows[:, s0 : s0 + count, starts[ch] : starts[ch] + width],
                 in_=res[:].rearrange("p (s n) -> p s n", s=count),
             )
 
+        def open_last(s):
+            ch = len(CHUNKS) - 1
+            bank = psum.tile([P, BANK], F32, name=("den", "num")[s % 2], bufs=(DEN_BUFS, NUM_BUFS)[s % 2])
+            mx(bank[:, 0 : CHUNKS[ch]], ("a", s), 0, ("e", ch, 0), 0, CHUNKS[ch], True, False)
+            banks["last", s] = bank
+
+        def close_last(s):
+            ch = len(CHUNKS) - 1
+            width = CHUNKS[ch]
+            bank = banks["last", s]
+            mx(bank[:, 0:width], ("a", s), P, ("e", ch, 1), 0, width, False, True)
+
+        def store_last(s):
+            ch = len(CHUNKS) - 1
+            width = CHUNKS[ch]
+            res = work.tile([P, BANK], F32, name="result", bufs=8)
+            (nc.vector.tensor_copy, nc.scalar.copy)[s % 2](out=res[:, 0:width], in_=banks["last", s][:, 0:width])
+            nc.sync.dma_start(out=out_rows[:, s, starts[ch] : starts[ch] + width], in_=res[:, 0:width])
+
         last = len(steps)
         slots = range(-4, last + 12)
         early_v = {i: [] for i in slots}
         first_v = {i: [] for i in slots}
         late_v = {i: [] for i in slots}
+        last_v = {i: [] for i in slots}
+        mid_v = {i: [] for i in slots}
+        window_slots = [W_FROM + PACK * k + PACK + WINDOW_LAG - 1 for k in range(len(POOL_TILES))] or [0]
         pe = {i: [] for i in slots}
         sc = {i: [] for i in slots}
 
@@ -250,15 +296,18 @@ def tile_dea_cross_efficiency_s7_kernel(tc, u, y, u0, v, x, a, out):
             pe[slot].append(lambda: turn_weight(name, b))
             if on_vector:
                 late_v[slot + 1].append(lambda: empty_weight(name, b, nc.vector.tensor_copy))
-                first_v[slot + 2].append(lambda: quantize((name, b), 2 * P))
+                early_v[slot + 2].append(lambda: quantize((name, b), 2 * P))
             else:
                 sc[slot + lag].append(lambda: empty_weight(name, b, nc.scalar.copy))
-                early_v[slot + lag + 1].append(lambda: quantize((name, b), 2 * P))
+                (first_v if name == "a" else early_v)[slot + lag + 1].append(lambda: quantize((name, b), 2 * P))
 
         def plan_data(panel, c, slot, share):
             late_v[slot].append(lambda: stage_data(panel, c, share))
             sc[slot].append(lambda: stage_data_scalar(panel, c, share))
-            first_v[slot + 1].append(lambda: quantize(("data", panel, c), PANEL))
+            if (panel, c) == (1, 2) and POOL_TILES:
+                last_v[window_slots[0] - 1].append(lambda: quantize(("data", panel, c), PANEL))
+            else:
+                first_v[slot + 1].append(lambda: quantize(("data", panel, c), PANEL))
 
         def plan_ratio(ch, g, slot):
             late_v[slot].append(lambda: stage_ratio(ch, g))
@@ -267,47 +316,94 @@ def tile_dea_cross_efficiency_s7_kernel(tc, u, y, u0, v, x, a, out):
         def plan_out(ch, s0, slot, on_vector):
             pe[slot].append(lambda: out_matmul(ch, s0))
             if on_vector:
-                late_v[slot + 1].append(lambda: store(ch, s0, nc.vector.tensor_copy))
+                vslot = min([w for w in window_slots if w > slot] + [slot + 1 if slot + 1 > window_slots[-1] else last])
+                mid_v[vslot].append(lambda: store(ch, s0, nc.vector.tensor_copy))
             else:
                 sc[slot + OUT_EVAC_LAG].append(lambda: store(ch, s0, nc.scalar.copy))
 
         plan_weight("v", 0, -4, 0)
+        def warm_up():
+            bank = psum.tile([P, BANK], F32, name="den", bufs=DEN_BUFS)
+            for n in range(WARM):
+                mx(bank[:, 0:256], ("v", 0), 0, ("v", 0), 0, 256, True, True)
+
+        if WARM:
+            pe[-3].append(warm_up)
         plan_data(0, 0, -4, S_SHARE_HEAD[0])
         plan_data(0, 1, -3, S_SHARE_HEAD[1])
-        plan_weight("v", 1, -2, 0)
+        plan_weight("v", 1, -2, 0, V_ON_V[1])
         plan_data(0, 2, Y_SLOT, S_SHARE_HEAD[2])
         for b in range(2, 8):
-            plan_weight("v", b, V_SLOTS[b], V_LAG)
+            plan_weight("v", b, V_SLOTS[b], V_LAG, V_ON_V[b])
         for b in range(4):
             plan_weight("u", b, U_SLOTS[b], U_LAG, U_ON_V[b])
         for b in range(4):
-            plan_weight("a", b, A_SLOT + b, 1)
-        for panel in range(1, panels):
-            for c in range(3):
-                plan_data(panel, c, XSLOTS[panel - 1][c], S_SHARE[panel - 1][c])
+            plan_weight("a", b, A_SLOT + b, 1, A_ON_V[b])
+        for panel, c, slot, share in OWN:
+            plan_data(panel, c, slot, share)
+
+        def plan_pool(k):
+            panel, c = POOL_TILES[k]
+            slot = window_slots[k]
+            if k == 0:
+                last_v[slot - 1].append(lambda: stage_data_gpsimd(panel, c))
+            if G_COLS < PANEL:
+                late_v[slot].append(lambda: interleave(nc.vector.tensor_copy, staged["data", panel, c], data_raw[panel, c], G_COLS, PANEL))
+            last_v[slot + Q_LAG].append(lambda: quantize(("data", panel, c), PANEL))
+            if k + 1 < len(POOL_TILES):
+                last_v[slot + Q_LAG].append(lambda: stage_data_gpsimd(*POOL_TILES[k + 1]))
+
+        for k in range(len(POOL_TILES)):
+            plan_pool(k)
+
+        windowed = W_FROM + PACK * len(POOL_TILES)
+        divide_slot = {}
+        num_slot = {}
+        for i in range(last):
+            if W_FROM <= i < windowed:
+                divide_slot[i] = PACK * (i // PACK) + PACK + WINDOW_LAG - 1
+                num_slot[i] = PACK * (i // PACK) + NUM_W[i % PACK]
+            else:
+                lag = STT_LAG0 if i < 4 else STT_LAG
+                divide_slot[i] = max(i + lag, divide_slot.get(i - 1, 0))
+                num_slot[i] = max(i + lag - 1, divide_slot.get(i - NUM_BUFS, 0))
         nout = 0
         for i, (ch, g, t0) in enumerate(steps):
             if t0 + BANK // CHUNKS[ch] == PACK:
-                plan_ratio(ch, g, i + STT_LAG + E_LAG)
-                if g == groups - 1:
+                plan_ratio(ch, g, divide_slot[i] + E_LAG)
+                if ch == len(CHUNKS) - 1:
+                    slot = divide_slot[i] + E_LAG + 1
+                    for s in range(PACK):
+                        if g == 0:
+                            pe[slot].append(lambda s=s: open_last(s))
+                        else:
+                            pe[slot].append(lambda s=s: close_last(s))
+                            sc[slot].append(lambda s=s: store_last(s))
+                elif g == groups - 1:
                     for n, s0 in enumerate(range(0, PACK, BANK // CHUNKS[ch])):
                         tail = ch == len(CHUNKS) - 1
-                        plan_out(ch, s0, i + STT_LAG + E_LAG + OUT_LAG + (0 if tail else n * OUT_STEP), nout in V_OUTS)
+                        plan_out(ch, s0, divide_slot[i] + E_LAG + (OUT_LAG_W if i < windowed else OUT_LAG) + (0 if tail else n * OUT_STEP), nout in V_OUTS)
                         nout = nout + 1
 
         for i in slots:
             for job in early_v[i]:
                 job()
-            if 0 <= i - STT_LAG < last:
-                divide(i - STT_LAG)
+            for n in range(last):
+                if divide_slot[n] == i:
+                    divide(n)
+            for job in mid_v[i]:
+                job()
             for job in first_v[i]:
                 job()
             for job in late_v[i]:
                 job()
+            for job in last_v[i]:
+                job()
             if 0 <= i + 1 < last:
                 den_matmul(i + 1)
-            if 0 <= i + 1 - NUM_LAG < last:
-                num_matmul(i + 1 - NUM_LAG)
+            for n in range(last):
+                if num_slot[n] == i:
+                    num_matmul(n)
             for job in pe[i]:
                 job()
             if 0 <= i < last:

@@ -18,48 +18,23 @@ P = 128
 PACK = 4
 K_PASS = P * PACK
 BANK = 512
+GROUPS = D // K_PASS
 PANEL = 512
-CHUNKS = (512,512,512,256,256)
-S_SHARE_HEAD = [128, 256, 0]
-OWN = [[1,0,1,64],[1,1,3,64],[1,2,5,64],[2,1,10,64],[3,1,18,64]]
-POOL_TILES = [(2,0),(2,2),(3,0),(3,2)]
-WINDOW_LAG = 2
-LOADS = [("v",0,1),("d",0,0,1),("d",0,1,1),("v",1,1),("d",0,2,1),("v",2,2),("u",0,2),("d",1,0,1),("v",4,2),("u",2,2),("v",6,2),("d",1,1,1),("d",1,2,1),("d",2,0,2),("d",2,1,2),("d",2,2,2),("a",0,4)]
-V_ON_V = [False,True]*4
-A_ON_V = [False]*4
-WARM = 0
-TAIL_SHARE = 0
-G_FIRST = 1
-Q_LAG = 3
-G_COLS = 416
-NUM_W = [3,3,4,4]
-OUT_LAG_W = 6
-W_FROM = 4
-TABLE_WARM = 0
-STT_LAG0 = 2
-STT_LAG = 3
-V_OUTS = []
-RECIP_BUFS = 6
-A_SLOT = 11
-OUT_LAG = 2
-OUT_STEP = 1
-OUT_EVAC_LAG = 1
-V_SLOTS = [0,0,-1,-1,1,1,3,3]
-V_LAG = 1
-U_SLOTS = [-1,0,2,4]
-U_LAG = 1
-U_ON_V = [False]*4
-Y_SLOT = -1
-E_LAG = 1
-DEN_BUFS = 2
-NUM_BUFS = 4
-AUX_BUFS = 2
+RUN = 4
+
+CHUNKS = (512, 512, 512, 256, 256)
+HEAD_SHARE = 192
+POOL_SHARE = 384
+FIRST_LAG, LAST_LAG = 2, 3
+OUT_LAG_RUNS, OUT_LAG = 6, 2
+
+DEN_BANKS, NUM_BANKS, AUX_BANKS = 2, 4, 2
+RECIP_TILES = 6
+RESULT_TILES = 8
 
 
 def tile_dea_cross_efficiency_s7_kernel(tc, u, y, u0, v, x, a, out):
     nc = tc.nc
-    groups = D // K_PASS
-    panels = J // PANEL
 
     with ExitStack() as ctx:
         keep = ctx.enter_context(tc.tile_pool(name="keep", bufs=1))
@@ -67,106 +42,111 @@ def tile_dea_cross_efficiency_s7_kernel(tc, u, y, u0, v, x, a, out):
         psum = ctx.enter_context(tc.psum_pool(name="psum", bufs=1))
         ctx.enter_context(tc.manual_schedule())
 
-        v_rows = v.rearrange("(g m t) k -> g m t k", g=groups, t=PACK)
-        u_rows = u.rearrange("(g m t) k -> g m t k", g=groups, t=PACK)
+        data_rows = {"x0": x[0:K_PASS, :], "x1": x[K_PASS : 2 * K_PASS, :], "y": y}
+        v_rows = v.rearrange("(g m t) k -> g m t k", g=GROUPS, t=PACK)
+        u_rows = u.rearrange("(g m t) k -> g m t k", g=GROUPS, t=PACK)
         a_rows = a.rearrange("(m s) d -> m s d", s=PACK)
         out_rows = out.rearrange("(m s) j -> m s j", s=PACK)
-        data_rows = [x[0:K_PASS, :], x[K_PASS : 2 * K_PASS, :], y]
+        data_raw, weight_words = {}, {}
 
-        data_raw, weight_raw = {}, {}
-
-        def load_data(panel, c, count):
-            raw = keep.tile([P, PACK, count * PANEL], BF16, name="data_raw_%d_%d" % (panel, c))
+        def load_data(part, panel, count):
+            raw = keep.tile([P, PACK, count * PANEL], BF16, name="raw_%s_%d" % (part, panel))
             cols = slice(panel * PANEL, (panel + count) * PANEL)
-            nc.sync.dma_start(out=raw[:], in_=data_rows[c][:, cols].rearrange("(p t) n -> p t n", t=PACK))
+            nc.sync.dma_start(out=raw[:], in_=data_rows[part][:, cols].rearrange("(p t) n -> p t n", t=PACK))
             for n in range(count):
-                data_raw[panel + n, c] = raw[:, :, n * PANEL : (n + 1) * PANEL]
+                data_raw[part, panel + n] = raw[:, :, n * PANEL : (n + 1) * PANEL]
 
-        def load_weight(name, rows, banks):
-            raw = keep.tile([P, len(banks) * 2 * K_PASS], BF16, name="raw_%s_%d" % (name, banks[0]))
+        def load_weights(name, first, count, rows):
+            raw = keep.tile([P, count * 2 * BANK], BF16, name="raw_%s_%d" % (name, first))
             nc.sync.dma_start(out=raw[:].rearrange("p (t k) -> p t k", t=rows.shape[1]), in_=rows)
             words = raw[:].bitcast(F32)
-            for n, bank in enumerate(banks):
-                weight_raw[name, bank] = words[:, n * BANK : (n + 1) * BANK]
+            for n in range(count):
+                weight_words[name, first + n] = words[:, n * BANK : (n + 1) * BANK]
 
-        bias = keep.tile([P, groups, PACK], BF16, name="bias")
-        nc.scalar.dma_start(out=bias[:], in_=u0.rearrange("(g p t) -> p g t", g=groups, t=PACK))
+        bias = keep.tile([P, GROUPS, PACK], BF16, name="bias")
 
-        for item in LOADS:
-            if item[0] == "v":
-                g, t0 = divmod(item[1], PACK)
-                load_weight("v", v_rows[g][:, t0 : t0 + item[2], :], list(range(item[1], item[1] + item[2])))
-            elif item[0] == "u":
-                g, t0 = divmod(2 * item[1], PACK)
-                load_weight("u", u_rows[g][:, t0 : t0 + 2 * item[2], :], list(range(item[1], item[1] + item[2])))
-            elif item[0] == "a":
-                load_weight("a", a_rows[:, item[1] : item[1] + item[2], :], list(range(item[1], item[1] + item[2])))
-            else:
-                load_data(item[1], item[2], item[3])
+        load_weights("v", 0, 1, v_rows[0][:, 0:1, :])
+        load_data("x0", 0, 1)
+        load_data("x1", 0, 1)
+        load_weights("v", 1, 1, v_rows[0][:, 1:2, :])
+        load_weights("v", 2, 2, v_rows[0][:, 2:4, :])
+        load_data("y", 0, 1)
+        load_weights("u", 0, 2, u_rows[0])
+        nc.sync.dma_start(out=bias[:], in_=u0.rearrange("(g p t) -> p g t", g=GROUPS, t=PACK))
+        load_data("x0", 1, 1)
+        load_weights("v", 4, 2, v_rows[1][:, 0:2, :])
+        load_weights("v", 6, 2, v_rows[1][:, 2:4, :])
+        load_data("x1", 1, 1)
+        load_weights("u", 2, 2, u_rows[1])
+        load_data("y", 1, 1)
+        load_data("x0", 2, 2)
+        load_data("x1", 2, 2)
+        load_weights("a", 0, 4, a_rows)
+        load_data("y", 2, 2)
 
         ident = keep.tile([P, P], F32, name="ident")
         make_identity(nc, ident[:])
-        if TABLE_WARM:
-            warm = keep.tile([P, 1], F32, name="warm")
-            nc.scalar.activation(out=warm[:], in_=ident[:, 0:1], func=ACT.Abs_reciprocal_sqrt, bias=1.0)
 
-        codes, scales, staged, banks = {}, {}, {}, {}
+        staged, codes, scales, banks = {}, {}, {}, {}
+        roots, recips, ratio_rows = {}, {}, {}
 
-        def aux_bank():
-            return psum.tile([P, BANK], F32, name="aux", bufs=AUX_BUFS)
+        def psum_bank(tag):
+            count = {"den": DEN_BANKS, "num": NUM_BANKS, "aux": AUX_BANKS}[tag]
+            return psum.tile([P, BANK], F32, name=tag, bufs=count)
 
         def quantize(key, width):
-            name = "_".join(str(part) for part in key)
-            code = keep.tile([P, width], U32, name="codes_" + name, align_bytes=64)
-            scale = keep.tile([P, width], U8, name="scales_" + name, align_bytes=64)
+            label = "_".join(str(item) for item in key)
+            code = keep.tile([P, width], U32, name="codes_" + label, align_bytes=64)
+            scale = keep.tile([P, width], U8, name="scales_" + label, align_bytes=64)
             nc.vector.quantize_mx(out=code[:].bitcast(FP8X4), scales=scale[:], in_=staged[key][:, 0 : PACK * width])
             codes[key], scales[key] = code, scale
 
-        def interleave(copy, dst, src, lo, hi):
+        def interleave(copy, dst, rows, lo, hi):
             copy(
-                out=dst[:, PACK * lo : PACK * hi].rearrange("p (c i t) -> p c t i", i=4, t=PACK),
-                in_=src[:, :, lo:hi].rearrange("p t (c i) -> p c t i", i=4),
+                out=dst[:, PACK * lo : PACK * hi].rearrange("p (c i t) -> p c t i", i=RUN, t=PACK),
+                in_=rows[:, :, lo:hi].rearrange("p t (c i) -> p c t i", i=RUN),
             )
 
-        def turn_weight(name, b):
-            bank = aux_bank() if name != "u" else psum.tile([P, BANK], F32, name="num", bufs=NUM_BUFS)
-            words = weight_raw[name, b]
-            for half in range(2):
+        def turn_weights(key):
+            bank = psum_bank("num" if key[0] == "u" else "aux")
+            half = BANK // 2
+            for h in range(2):
                 for w in range(2):
-                    col = (2 * half + w) * P
-                    nc.tensor.transpose(
-                        bank[:, col : col + P], words[:, 256 * half + w : 256 * (half + 1) : 2], ident[:]
-                    )
-            banks[name, b] = bank
+                    col = (2 * h + w) * P
+                    words = weight_words[key][:, half * h + w : half * (h + 1) : 2]
+                    nc.tensor.transpose(bank[:, col : col + P], words, ident[:])
+            banks[key] = bank
 
-        def empty_weight(name, b, copy):
+        def stage_weights(key, copy):
             dst = work.tile([P, 2 * K_PASS], BF16, name="weight_staged", align_bytes=64)
             copy(
                 out=dst[:].bitcast(F32).rearrange("p (h m w) -> p h m w", h=2, w=2),
-                in_=banks[name, b][:].rearrange("p (h w m) -> p h m w", h=2, w=2),
+                in_=banks[key][:].rearrange("p (h w m) -> p h m w", h=2, w=2),
             )
-            staged[name, b] = dst
+            staged[key] = dst
 
-        def stage_data(panel, c, share):
-            if (panel, c) == (1, 2) and POOL_TILES:
-                dst = work.tile([P, PACK * PANEL], BF16, name="pool_staged", bufs=1, align_bytes=64)
+        def shared_tile():
+            return work.tile([P, PACK * PANEL], BF16, name="shared_staged", bufs=1, align_bytes=64)
+
+        def stage_data(key, first_col, through_shared):
+            if through_shared:
+                dst = shared_tile()
             else:
                 dst = work.tile([P, PACK * PANEL], BF16, name="data_staged", align_bytes=64)
-            staged["data", panel, c] = dst
-            interleave(nc.vector.tensor_copy, dst, data_raw[panel, c], share, PANEL)
+            staged[key] = dst
+            interleave(nc.vector.tensor_copy, dst, data_raw[key], first_col, PANEL)
 
-        def stage_data_gpsimd(panel, c):
-            dst = work.tile([P, PACK * PANEL], BF16, name="pool_staged", bufs=1, align_bytes=64)
-            staged["data", panel, c] = dst
+        def stage_data_gpsimd(key):
+            dst = shared_tile()
+            staged[key] = dst
             nc.gpsimd.tensor_scalar(
-                out=dst[:, 0 : PACK * G_COLS].rearrange("p (n t) -> p n t", t=PACK),
-                in0=data_raw[panel, c][:, :, 0:G_COLS].rearrange("p t n -> p n t"),
-                scalar1=1.0, scalar2=0.0, op0=ALU.mult, op1=ALU.add,
+                out=dst[:, 0 : PACK * POOL_SHARE].rearrange("p (n t) -> p n t", t=PACK),
+                in0=data_raw[key][:, :, 0:POOL_SHARE].rearrange("p t n -> p n t"),
+                scalar1=1.0,
+                scalar2=0.0,
+                op0=ALU.mult,
+                op1=ALU.add,
             )
-
-        def stage_data_scalar(panel, c, share):
-            if share:
-                interleave(nc.scalar.copy, staged["data", panel, c], data_raw[panel, c], 0, share)
 
         def mx(acc, left, left_col, right, right_col, width, start, stop):
             lcols = slice(left_col, left_col + P)
@@ -182,33 +162,33 @@ def tile_dea_cross_efficiency_s7_kernel(tc, u, y, u0, v, x, a, out):
             )
 
         starts = [sum(CHUNKS[:n]) for n in range(len(CHUNKS))]
-        steps = []
-        for ch, width in enumerate(CHUNKS):
-            for g in range(groups):
-                for t0 in range(0, PACK, BANK // width):
-                    steps.append((ch, g, t0))
-        roots, recips, ratio = {}, {}, {}
+        last_chunk = len(CHUNKS) - 1
+        steps = [
+            (ch, g, t0)
+            for ch, width in enumerate(CHUNKS)
+            for g in range(GROUPS)
+            for t0 in range(0, PACK, BANK // width)
+        ]
 
         def den_matmul(i):
             ch, g, t0 = steps[i]
             width = CHUNKS[ch]
             panel, col = divmod(starts[ch], PANEL)
-            bank = psum.tile([P, BANK], F32, name="den", bufs=DEN_BUFS)
+            bank = psum_bank("den")
             for n in range(BANK // width):
-                for c in range(2):
-                    mx(bank[:, n * width : (n + 1) * width], ("v", PACK * g + t0 + n), c * P,
-                       ("data", panel, c), col, width, c == 0, c == 1)
+                for c, part in enumerate(("x0", "x1")):
+                    acc = bank[:, n * width : (n + 1) * width]
+                    mx(acc, ("v", PACK * g + t0 + n), c * P, (part, panel), col, width, c == 0, c == 1)
             banks["den", i] = bank
 
         def num_matmul(i):
             ch, g, t0 = steps[i]
             width = CHUNKS[ch]
             panel, col = divmod(starts[ch], PANEL)
-            bank = psum.tile([P, BANK], F32, name="num", bufs=NUM_BUFS)
+            bank = psum_bank("num")
             for n in range(BANK // width):
-                pair, half = divmod(PACK * g + t0 + n, 2)
-                mx(bank[:, n * width : (n + 1) * width], ("u", pair), half * P,
-                   ("data", panel, 2), col, width, True, True)
+                pair, h = divmod(PACK * g + t0 + n, 2)
+                mx(bank[:, n * width : (n + 1) * width], ("u", pair), h * P, ("y", panel), col, width, True, True)
             banks["num", i] = bank
 
         def root(i):
@@ -217,198 +197,142 @@ def tile_dea_cross_efficiency_s7_kernel(tc, u, y, u0, v, x, a, out):
             roots[i] = r
 
         def square(i):
-            r2 = work.tile([P, BANK], F32, name="recip", bufs=RECIP_BUFS)
-            nc.scalar.activation(out=r2[:], in_=roots[i][:], func=ACT.Square)
-            recips[i] = r2
+            recip = work.tile([P, BANK], F32, name="recip", bufs=RECIP_TILES)
+            nc.scalar.activation(out=recip[:], in_=roots[i][:], func=ACT.Square)
+            recips[i] = recip
 
         def divide(i):
             ch, g, t0 = steps[i]
             width = CHUNKS[ch]
             if t0 == 0:
                 rows = work.tile([P, PACK * PANEL], BF16, name="ratio_rows", bufs=2)
-                ratio[ch, g] = rows[:, 0 : PACK * width].rearrange("p (t n) -> p t n", t=PACK)
+                ratio_rows[ch, g] = rows[:, 0 : PACK * width].rearrange("p (t n) -> p t n", t=PACK)
             for n in range(BANK // width):
                 cols = slice(n * width, (n + 1) * width)
                 nc.vector.scalar_tensor_tensor(
-                    out=ratio[ch, g][:, t0 + n, :], in0=banks["num", i][:, cols],
-                    scalar=bias[:, g, t0 + n : t0 + n + 1], in1=recips[i][:, cols],
-                    op0=ALU.add, op1=ALU.mult,
+                    out=ratio_rows[ch, g][:, t0 + n, :],
+                    in0=banks["num", i][:, cols],
+                    scalar=bias[:, g, t0 + n : t0 + n + 1],
+                    in1=recips[i][:, cols],
+                    op0=ALU.add,
+                    op1=ALU.mult,
                 )
 
         def stage_ratio(ch, g):
             dst = work.tile([P, PACK * PANEL], BF16, name="ratio_staged", bufs=2, align_bytes=64)
             staged["e", ch, g] = dst
-            share = TAIL_SHARE if (ch, g) == (len(CHUNKS) - 1, groups - 1) else 0
-            if share:
-                interleave(nc.scalar.copy, dst, ratio[ch, g], 0, share)
-            interleave(nc.vector.tensor_copy, dst, ratio[ch, g], share, CHUNKS[ch])
+            interleave(nc.vector.tensor_copy, dst, ratio_rows[ch, g], 0, CHUNKS[ch])
 
         def out_matmul(ch, s0):
             width = CHUNKS[ch]
-            bank = aux_bank()
+            bank = psum_bank("aux")
             for n in range(BANK // width):
-                for g in range(groups):
-                    mx(bank[:, n * width : (n + 1) * width], ("a", s0 + n), g * P,
-                       ("e", ch, g), 0, width, g == 0, g == groups - 1)
+                for g in range(GROUPS):
+                    acc = bank[:, n * width : (n + 1) * width]
+                    mx(acc, ("a", s0 + n), g * P, ("e", ch, g), 0, width, g == 0, g == GROUPS - 1)
             banks["out", ch, s0] = bank
 
-        def store(ch, s0, copy):
+        def last_out_pass(s, g):
+            width = CHUNKS[last_chunk]
+            if g == 0:
+                banks["out", last_chunk, s] = psum_bank(("den", "num")[s % 2])
+            acc = banks["out", last_chunk, s][:, 0:width]
+            mx(acc, ("a", s), g * P, ("e", last_chunk, g), 0, width, g == 0, g == GROUPS - 1)
+
+        def store(ch, s0, count, copy):
             width = CHUNKS[ch]
-            count = BANK // width
-            res = work.tile([P, BANK], F32, name="result", bufs=8)
-            copy(out=res[:], in_=banks["out", ch, s0][:])
+            result = work.tile([P, BANK], F32, name="result", bufs=RESULT_TILES)
+            copy(out=result[:, 0 : count * width], in_=banks["out", ch, s0][:, 0 : count * width])
             nc.sync.dma_start(
                 out=out_rows[:, s0 : s0 + count, starts[ch] : starts[ch] + width],
-                in_=res[:].rearrange("p (s n) -> p s n", s=count),
+                in_=result[:, 0 : count * width].rearrange("p (s n) -> p s n", s=count),
             )
 
-        def open_last(s):
-            ch = len(CHUNKS) - 1
-            bank = psum.tile([P, BANK], F32, name=("den", "num")[s % 2], bufs=(DEN_BUFS, NUM_BUFS)[s % 2])
-            mx(bank[:, 0 : CHUNKS[ch]], ("a", s), 0, ("e", ch, 0), 0, CHUNKS[ch], True, False)
-            banks["last", s] = bank
+        phases = ("urgent", "divide", "quantize", "interleave", "hand over", "den", "num", "tensor", "root", "scalar")
+        table = {}
 
-        def close_last(s):
-            ch = len(CHUNKS) - 1
-            width = CHUNKS[ch]
-            bank = banks["last", s]
-            mx(bank[:, 0:width], ("a", s), P, ("e", ch, 1), 0, width, False, True)
+        def plan(slot, phase, job, *args):
+            table.setdefault((slot, phase), []).append((job, args))
 
-        def store_last(s):
-            ch = len(CHUNKS) - 1
-            width = CHUNKS[ch]
-            res = work.tile([P, BANK], F32, name="result", bufs=8)
-            (nc.vector.tensor_copy, nc.scalar.copy)[s % 2](out=res[:, 0:width], in_=banks["last", s][:, 0:width])
-            nc.sync.dma_start(out=out_rows[:, s, starts[ch] : starts[ch] + width], in_=res[:, 0:width])
+        def plan_weights(key, slot, wait):
+            plan(slot, "tensor", turn_weights, key)
+            plan(slot + wait, "scalar", stage_weights, key, nc.scalar.copy)
+            plan(slot + wait + 1, "quantize" if key[0] == "a" else "urgent", quantize, key, 2 * P)
 
-        last = len(steps)
-        slots = range(-4, last + 12)
-        early_v = {i: [] for i in slots}
-        first_v = {i: [] for i in slots}
-        late_v = {i: [] for i in slots}
-        last_v = {i: [] for i in slots}
-        mid_v = {i: [] for i in slots}
-        window_slots = [W_FROM + PACK * k + PACK + WINDOW_LAG - 1 for k in range(len(POOL_TILES))] or [0]
-        pe = {i: [] for i in slots}
-        sc = {i: [] for i in slots}
+        def plan_data(key, slot, scalar_cols):
+            plan(slot, "interleave", stage_data, key, scalar_cols, False)
+            if scalar_cols:
+                plan(slot, "scalar", lambda: interleave(nc.scalar.copy, staged[key], data_raw[key], 0, scalar_cols))
+            plan(slot + 1, "quantize", quantize, key, PANEL)
 
-        def plan_weight(name, b, slot, lag, on_vector=False):
-            pe[slot].append(lambda: turn_weight(name, b))
-            if on_vector:
-                late_v[slot + 1].append(lambda: empty_weight(name, b, nc.vector.tensor_copy))
-                early_v[slot + 2].append(lambda: quantize((name, b), 2 * P))
-            else:
-                sc[slot + lag].append(lambda: empty_weight(name, b, nc.scalar.copy))
-                (first_v if name == "a" else early_v)[slot + lag + 1].append(lambda: quantize((name, b), 2 * P))
+        plan_weights(("v", 0), -4, 0)
+        plan_data(("x0", 0), -4, HEAD_SHARE)
+        plan_data(("x1", 0), -3, HEAD_SHARE)
+        plan_weights(("v", 1), -2, 0)
+        plan_data(("y", 0), -1, 0)
+        plan(-2, "tensor", turn_weights, ("v", 2))
+        plan(-1, "interleave", stage_weights, ("v", 2), nc.vector.tensor_copy)
+        plan(0, "urgent", quantize, ("v", 2), 2 * P)
+        plan_weights(("v", 3), -1, 1)
+        for b in range(PACK, 2 * PACK):
+            plan_weights(("v", b), b - b % 2 - 3, 1)
+        for b in range(2):
+            plan_weights(("u", b), b - 1, 1)
+            plan_weights(("u", 2 + b), PACK + b, 1)
 
-        def plan_data(panel, c, slot, share):
-            late_v[slot].append(lambda: stage_data(panel, c, share))
-            sc[slot].append(lambda: stage_data_scalar(panel, c, share))
-            if (panel, c) == (1, 2) and POOL_TILES:
-                last_v[window_slots[0] - 1].append(lambda: quantize(("data", panel, c), PANEL))
-            else:
-                first_v[slot + 1].append(lambda: quantize(("data", panel, c), PANEL))
+        pool_tiles = [(part, panel) for panel in (2, 3) for part in ("x0", "y")]
+        runs = [PACK * (k + 2) + 1 for k in range(len(pool_tiles))]
+        in_runs = range(PACK, PACK * (len(runs) + 1))
 
-        def plan_ratio(ch, g, slot):
-            late_v[slot].append(lambda: stage_ratio(ch, g))
-            first_v[slot + 1].append(lambda: quantize(("e", ch, g), CHUNKS[ch]))
+        for s in range(PACK):
+            plan_weights(("a", s), runs[0] + 1 + s, 1)
 
-        def plan_out(ch, s0, slot, on_vector):
-            pe[slot].append(lambda: out_matmul(ch, s0))
-            if on_vector:
-                vslot = min([w for w in window_slots if w > slot] + [slot + 1 if slot + 1 > window_slots[-1] else last])
-                mid_v[vslot].append(lambda: store(ch, s0, nc.vector.tensor_copy))
-            else:
-                sc[slot + OUT_EVAC_LAG].append(lambda: store(ch, s0, nc.scalar.copy))
+        plan_data(("x0", 1), 1, 0)
+        plan_data(("x1", 1), 3, 0)
+        plan(5, "interleave", stage_data, ("y", 1), 0, True)
+        plan(runs[0] - 1, "hand over", quantize, ("y", 1), PANEL)
+        plan_data(("x1", 2), runs[0] + 1, 0)
+        plan_data(("x1", 3), runs[2] + 1, 0)
 
-        plan_weight("v", 0, -4, 0)
-        def warm_up():
-            bank = psum.tile([P, BANK], F32, name="den", bufs=DEN_BUFS)
-            for n in range(WARM):
-                mx(bank[:, 0:256], ("v", 0), 0, ("v", 0), 0, 256, True, True)
+        def plan_pool_tile(key, slot):
+            plan(slot - 1, "hand over", stage_data_gpsimd, key)
+            plan(slot, "interleave",
+                 lambda: interleave(nc.vector.tensor_copy, staged[key], data_raw[key], POOL_SHARE, PANEL))
+            plan(slot + PACK - 1, "hand over", quantize, key, PANEL)
 
-        if WARM:
-            pe[-3].append(warm_up)
-        plan_data(0, 0, -4, S_SHARE_HEAD[0])
-        plan_data(0, 1, -3, S_SHARE_HEAD[1])
-        plan_weight("v", 1, -2, 0, V_ON_V[1])
-        plan_data(0, 2, Y_SLOT, S_SHARE_HEAD[2])
-        for b in range(2, 8):
-            plan_weight("v", b, V_SLOTS[b], V_LAG, V_ON_V[b])
-        for b in range(4):
-            plan_weight("u", b, U_SLOTS[b], U_LAG, U_ON_V[b])
-        for b in range(4):
-            plan_weight("a", b, A_SLOT + b, 1, A_ON_V[b])
-        for panel, c, slot, share in OWN:
-            plan_data(panel, c, slot, share)
+        for key, slot in zip(pool_tiles, runs):
+            plan_pool_tile(key, slot)
 
-        def plan_pool(k):
-            panel, c = POOL_TILES[k]
-            slot = window_slots[k]
-            if k == 0:
-                last_v[slot - 1].append(lambda: stage_data_gpsimd(panel, c))
-            if G_COLS < PANEL:
-                late_v[slot].append(lambda: interleave(nc.vector.tensor_copy, staged["data", panel, c], data_raw[panel, c], G_COLS, PANEL))
-            last_v[slot + Q_LAG].append(lambda: quantize(("data", panel, c), PANEL))
-            if k + 1 < len(POOL_TILES):
-                last_v[slot + Q_LAG].append(lambda: stage_data_gpsimd(*POOL_TILES[k + 1]))
-
-        for k in range(len(POOL_TILES)):
-            plan_pool(k)
-
-        windowed = W_FROM + PACK * len(POOL_TILES)
-        divide_slot = {}
-        num_slot = {}
-        for i in range(last):
-            if W_FROM <= i < windowed:
-                divide_slot[i] = PACK * (i // PACK) + PACK + WINDOW_LAG - 1
-                num_slot[i] = PACK * (i // PACK) + NUM_W[i % PACK]
-            else:
-                lag = STT_LAG0 if i < 4 else STT_LAG
-                divide_slot[i] = max(i + lag, divide_slot.get(i - 1, 0))
-                num_slot[i] = max(i + lag - 1, divide_slot.get(i - NUM_BUFS, 0))
-        nout = 0
         for i, (ch, g, t0) in enumerate(steps):
-            if t0 + BANK // CHUNKS[ch] == PACK:
-                plan_ratio(ch, g, divide_slot[i] + E_LAG)
-                if ch == len(CHUNKS) - 1:
-                    slot = divide_slot[i] + E_LAG + 1
+            plan(i - 1, "den", den_matmul, i)
+            plan(i, "root", root, i)
+            if i in in_runs:
+                divide_slot = runs[i // PACK - 1]
+                plan(divide_slot - 2 + t0 // 2, "num", num_matmul, i)
+            else:
+                divide_slot = i + (FIRST_LAG if i < PACK else LAST_LAG)
+                plan(divide_slot - 1, "num", num_matmul, i)
+            plan(divide_slot, "divide", divide, i)
+            per_bank = BANK // CHUNKS[ch]
+            if t0 + per_bank == PACK:
+                plan(divide_slot + 1, "interleave", stage_ratio, ch, g)
+                plan(divide_slot + 2, "quantize", quantize, ("e", ch, g), CHUNKS[ch])
+                if ch == last_chunk:
                     for s in range(PACK):
-                        if g == 0:
-                            pe[slot].append(lambda s=s: open_last(s))
-                        else:
-                            pe[slot].append(lambda s=s: close_last(s))
-                            sc[slot].append(lambda s=s: store_last(s))
-                elif g == groups - 1:
-                    for n, s0 in enumerate(range(0, PACK, BANK // CHUNKS[ch])):
-                        tail = ch == len(CHUNKS) - 1
-                        plan_out(ch, s0, divide_slot[i] + E_LAG + (OUT_LAG_W if i < windowed else OUT_LAG) + (0 if tail else n * OUT_STEP), nout in V_OUTS)
-                        nout = nout + 1
+                        plan(divide_slot + 2, "tensor", last_out_pass, s, g)
+                        if g == GROUPS - 1:
+                            copy = (nc.vector.tensor_copy, nc.scalar.copy)[s % 2]
+                            plan(divide_slot + 2, "scalar", store, ch, s, 1, copy)
+                elif g == GROUPS - 1:
+                    first = divide_slot + 1 + (OUT_LAG_RUNS if i in in_runs else OUT_LAG)
+                    for n, s0 in enumerate(range(0, PACK, per_bank)):
+                        plan(first + n, "tensor", out_matmul, ch, s0)
+                        plan(first + n + 1, "scalar", store, ch, s0, per_bank, nc.scalar.copy)
+        for i in range(len(steps)):
+            plan(i + 1, "root", square, i)
 
-        for i in slots:
-            for job in early_v[i]:
-                job()
-            for n in range(last):
-                if divide_slot[n] == i:
-                    divide(n)
-            for job in mid_v[i]:
-                job()
-            for job in first_v[i]:
-                job()
-            for job in late_v[i]:
-                job()
-            for job in last_v[i]:
-                job()
-            if 0 <= i + 1 < last:
-                den_matmul(i + 1)
-            for n in range(last):
-                if num_slot[n] == i:
-                    num_matmul(n)
-            for job in pe[i]:
-                job()
-            if 0 <= i < last:
-                root(i)
-            if 0 <= i - 1 < last:
-                square(i - 1)
-            for job in sc[i]:
-                job()
+        slots = sorted({slot for slot, phase in table})
+        for slot in slots:
+            for phase in phases:
+                for job, args in table.get((slot, phase), []):
+                    job(*args)

@@ -20,7 +20,7 @@ K_PASS = P * PACK
 BANK = 512
 GROUPS = D // K_PASS
 PANEL = 512
-RUN = 4
+RUN = 8
 
 CHUNKS = (512, 512, 512, 256, 256)
 HEAD_SHARE = 192

@@ -26,7 +26,7 @@ CHUNKS = (512, 512, 512, 256, 256)
 HEAD_SHARE = 192
 POOL_SHARE = 384
 FIRST_LAG, LAST_LAG = 2, 3
-OUT_LAG_RUNS, OUT_LAG = 6, 2
+OUT_LAGS = (6, 4, 2, 2)
 
 DEN_BANKS, NUM_BANKS, AUX_BANKS = 2, 4, 2
 RECIP_TILES = 6
@@ -136,12 +136,15 @@ def tile_dea_cross_efficiency_s7_kernel(tc, u, y, u0, v, x, a, out):
             staged[key] = dst
             interleave(nc.vector.tensor_copy, dst, data_raw[key], first_col, PANEL)
 
-        def stage_data_gpsimd(key):
+        def source_rows(key):
+            return ratio_rows[key[1:]] if key[0] == "e" else data_raw[key]
+
+        def stage_gpsimd(key):
             dst = shared_tile()
             staged[key] = dst
             nc.gpsimd.tensor_scalar(
                 out=dst[:, 0 : PACK * POOL_SHARE].rearrange("p (n t) -> p n t", t=PACK),
-                in0=data_raw[key][:, :, 0:POOL_SHARE].rearrange("p t n -> p n t"),
+                in0=source_rows(key)[:, :, 0:POOL_SHARE].rearrange("p t n -> p n t"),
                 scalar1=1.0,
                 scalar2=0.0,
                 op0=ALU.mult,
@@ -280,7 +283,8 @@ def tile_dea_cross_efficiency_s7_kernel(tc, u, y, u0, v, x, a, out):
             plan_weights(("u", b), b - 1, 1)
             plan_weights(("u", 2 + b), PACK + b, 1)
 
-        pool_tiles = [(part, panel) for panel in (2, 3) for part in ("x0", "y")]
+        late_ratio = ("e", 2, 0)
+        pool_tiles = [(part, panel) for panel in (2, 3) for part in ("x0", "y")] + [late_ratio]
         runs = [PACK * (k + 2) + 1 for k in range(len(pool_tiles))]
         in_runs = range(PACK, PACK * (len(runs) + 1))
 
@@ -295,10 +299,10 @@ def tile_dea_cross_efficiency_s7_kernel(tc, u, y, u0, v, x, a, out):
         plan_data(("x1", 3), runs[2] + 1, 0)
 
         def plan_pool_tile(key, slot):
-            plan(slot - 1, "hand over", stage_data_gpsimd, key)
+            plan(slot - 1, "hand over", stage_gpsimd, key)
             plan(slot, "interleave",
-                 lambda: interleave(nc.vector.tensor_copy, staged[key], data_raw[key], POOL_SHARE, PANEL))
-            plan(slot + PACK - 1, "hand over", quantize, key, PANEL)
+                 lambda: interleave(nc.vector.tensor_copy, staged[key], source_rows(key), POOL_SHARE, PANEL))
+            plan(slot if key == late_ratio else slot + PACK - 1, "hand over", quantize, key, PANEL)
 
         for key, slot in zip(pool_tiles, runs):
             plan_pool_tile(key, slot)
@@ -311,12 +315,14 @@ def tile_dea_cross_efficiency_s7_kernel(tc, u, y, u0, v, x, a, out):
                 plan(divide_slot - 2 + t0 // 2, "num", num_matmul, i)
             else:
                 divide_slot = i + (FIRST_LAG if i < PACK else LAST_LAG)
-                plan(divide_slot - 1, "num", num_matmul, i)
+                plan(i + 1, "num", num_matmul, i)
             plan(divide_slot, "divide", divide, i)
             per_bank = BANK // CHUNKS[ch]
             if t0 + per_bank == PACK:
-                plan(divide_slot + 1, "interleave", stage_ratio, ch, g)
-                plan(divide_slot + 2, "quantize", quantize, ("e", ch, g), CHUNKS[ch])
+                if ("e", ch, g) != late_ratio:
+                    stage_slot = divide_slot if divide_slot == runs[-1] else divide_slot + 1
+                    plan(stage_slot, "interleave", stage_ratio, ch, g)
+                    plan(stage_slot + 1, "quantize", quantize, ("e", ch, g), CHUNKS[ch])
                 if ch == last_chunk:
                     for s in range(PACK):
                         plan(divide_slot + 2, "tensor", last_out_pass, s, g)
@@ -324,10 +330,13 @@ def tile_dea_cross_efficiency_s7_kernel(tc, u, y, u0, v, x, a, out):
                             copy = (nc.vector.tensor_copy, nc.scalar.copy)[s % 2]
                             plan(divide_slot + 2, "scalar", store, ch, s, 1, copy)
                 elif g == GROUPS - 1:
-                    first = divide_slot + 1 + (OUT_LAG_RUNS if i in in_runs else OUT_LAG)
+                    first = divide_slot + 1 + OUT_LAGS[ch]
                     for n, s0 in enumerate(range(0, PACK, per_bank)):
                         plan(first + n, "tensor", out_matmul, ch, s0)
-                        plan(first + n + 1, "scalar", store, ch, s0, per_bank, nc.scalar.copy)
+                        if (ch, s0) == (1, 0):
+                            plan(first + n + 1, "interleave", store, ch, s0, per_bank, nc.vector.tensor_copy)
+                        else:
+                            plan(first + n + 1, "scalar", store, ch, s0, per_bank, nc.scalar.copy)
         for i in range(len(steps)):
             plan(i + 1, "root", square, i)
 

from contextlib import ExitStack

import concourse.mybir as mybir
from concourse.masks import make_identity

D, J, KO, KI, Q = 1024, 2048, 512, 1024, 512
FLOPS = 2 * J * (D * KO + D * KI + Q * D)

F32 = mybir.dt.float32
BF16 = mybir.dt.bfloat16
U32 = mybir.dt.uint32
U8 = mybir.dt.uint8
FP8X4 = mybir.dt.float8_e4m3fn_x4
ACT = mybir.ActivationFunctionType
ALU = mybir.AluOpType

P = 128
PACK = 4
K_PASS = P * PACK
BANK = 512
GROUPS = D // K_PASS
PANEL = 512
RUN = 8

CHUNKS = (512, 512, 512, 256, 256)
HEAD_SHARE = 192
POOL_SHARE = 384
FIRST_LAG, LAST_LAG = 2, 3
OUT_LAGS = (6, 4, 2, 2)

DEN_BANKS, NUM_BANKS, AUX_BANKS = 2, 4, 2
RECIP_TILES = 6
RESULT_TILES = 8


def tile_dea_cross_efficiency_s7_kernel(tc, u, y, u0, v, x, a, out):
    nc = tc.nc

    with ExitStack() as ctx:
        keep = ctx.enter_context(tc.tile_pool(name="keep", bufs=1))
        work = ctx.enter_context(tc.tile_pool(name="work", bufs=3))
        psum = ctx.enter_context(tc.psum_pool(name="psum", bufs=1))
        ctx.enter_context(tc.manual_schedule())

        data_rows = {"x0": x[0:K_PASS, :], "x1": x[K_PASS : 2 * K_PASS, :], "y": y}
        v_rows = v.rearrange("(g m t) k -> g m t k", g=GROUPS, t=PACK)
        u_rows = u.rearrange("(g m t) k -> g m t k", g=GROUPS, t=PACK)
        a_rows = a.rearrange("(m s) d -> m s d", s=PACK)
        out_rows = out.rearrange("(m s) j -> m s j", s=PACK)
        data_raw, weight_words = {}, {}

        def load_data(part, panel, count):
            raw = keep.tile([P, PACK, count * PANEL], BF16, name="raw_%s_%d" % (part, panel))
            cols = slice(panel * PANEL, (panel + count) * PANEL)
            nc.sync.dma_start(out=raw[:], in_=data_rows[part][:, cols].rearrange("(p t) n -> p t n", t=PACK))
            for n in range(count):
                data_raw[part, panel + n] = raw[:, :, n * PANEL : (n + 1) * PANEL]

        def load_weights(name, first, count, rows):
            raw = keep.tile([P, count * 2 * BANK], BF16, name="raw_%s_%d" % (name, first))
            nc.sync.dma_start(out=raw[:].rearrange("p (t k) -> p t k", t=rows.shape[1]), in_=rows)
            words = raw[:].bitcast(F32)
            for n in range(count):
                weight_words[name, first + n] = words[:, n * BANK : (n + 1) * BANK]

        bias = keep.tile([P, GROUPS, PACK], BF16, name="bias")

        load_weights("v", 0, 1, v_rows[0][:, 0:1, :])
        load_data("x0", 0, 1)
        load_data("x1", 0, 1)
        load_weights("v", 1, 1, v_rows[0][:, 1:2, :])
        load_weights("v", 2, 2, v_rows[0][:, 2:4, :])
        load_data("y", 0, 1)
        load_weights("u", 0, 2, u_rows[0])
        nc.sync.dma_start(out=bias[:], in_=u0.rearrange("(g p t) -> p g t", g=GROUPS, t=PACK))
        load_data("x0", 1, 1)
        load_weights("v", 4, 2, v_rows[1][:, 0:2, :])
        load_weights("v", 6, 2, v_rows[1][:, 2:4, :])
        load_data("x1", 1, 1)
        load_weights("u", 2, 2, u_rows[1])
        load_data("y", 1, 1)
        load_data("x0", 2, 2)
        load_data("x1", 2, 2)
        load_weights("a", 0, 4, a_rows)
        load_data("y", 2, 2)

        ident = keep.tile([P, P], F32, name="ident")
        make_identity(nc, ident[:])

        staged, codes, scales, banks = {}, {}, {}, {}
        roots, recips, ratio_rows = {}, {}, {}

        def psum_bank(tag):
            count = {"den": DEN_BANKS, "num": NUM_BANKS, "aux": AUX_BANKS}[tag]
            return psum.tile([P, BANK], F32, name=tag, bufs=count)

        def quantize(key, width):
            label = "_".join(str(item) for item in key)
            code = keep.tile([P, width], U32, name="codes_" + label, align_bytes=64)
            scale = keep.tile([P, width], U8, name="scales_" + label, align_bytes=64)
            nc.vector.quantize_mx(out=code[:].bitcast(FP8X4), scales=scale[:], in_=staged[key][:, 0 : PACK * width])
            codes[key], scales[key] = code, scale

        def interleave(copy, dst, rows, lo, hi):
            copy(
                out=dst[:, PACK * lo : PACK * hi].rearrange("p (c i t) -> p c t i", i=RUN, t=PACK),
                in_=rows[:, :, lo:hi].rearrange("p t (c i) -> p c t i", i=RUN),
            )

        def turn_weights(key):
            bank = psum_bank("num" if key[0] == "u" else "aux")
            half = BANK // 2
            for h in range(2):
                for w in range(2):
                    col = (2 * h + w) * P
                    words = weight_words[key][:, half * h + w : half * (h + 1) : 2]
                    nc.tensor.transpose(bank[:, col : col + P], words, ident[:])
            banks[key] = bank

        def stage_weights(key, copy):
            dst = work.tile([P, 2 * K_PASS], BF16, name="weight_staged", align_bytes=64)
            copy(
                out=dst[:].bitcast(F32).rearrange("p (h m w) -> p h m w", h=2, w=2),
                in_=banks[key][:].rearrange("p (h w m) -> p h m w", h=2, w=2),
            )
            staged[key] = dst

        def shared_tile():
            return work.tile([P, PACK * PANEL], BF16, name="shared_staged", bufs=1, align_bytes=64)

        def stage_data(key, first_col, through_shared):
            if through_shared:
                dst = shared_tile()
            else:
                dst = work.tile([P, PACK * PANEL], BF16, name="data_staged", align_bytes=64)
            staged[key] = dst
            interleave(nc.vector.tensor_copy, dst, data_raw[key], first_col, PANEL)

        def source_rows(key):
            return ratio_rows[key[1:]] if key[0] == "e" else data_raw[key]

        def stage_gpsimd(key):
            dst = shared_tile()
            staged[key] = dst
            nc.gpsimd.tensor_scalar(
                out=dst[:, 0 : PACK * POOL_SHARE].rearrange("p (n t) -> p n t", t=PACK),
                in0=source_rows(key)[:, :, 0:POOL_SHARE].rearrange("p t n -> p n t"),
                scalar1=1.0,
                scalar2=0.0,
                op0=ALU.mult,
                op1=ALU.add,
            )

        def mx(acc, left, left_col, right, right_col, width, start, stop):
            lcols = slice(left_col, left_col + P)
            rcols = slice(right_col, right_col + width)
            nc.tensor.matmul_mx(
                out=acc,
                lhsT=codes[left][:, lcols].bitcast(FP8X4),
                lhsT_scale=scales[left][:, lcols],
                rhs=codes[right][:, rcols].bitcast(FP8X4),
                rhs_scale=scales[right][:, rcols],
                start=start,
                stop=stop,
            )

        starts = [sum(CHUNKS[:n]) for n in range(len(CHUNKS))]
        last_chunk = len(CHUNKS) - 1
        steps = [
            (ch, g, t0)
            for ch, width in enumerate(CHUNKS)
            for g in range(GROUPS)
            for t0 in range(0, PACK, BANK // width)
        ]

        def den_matmul(i):
            ch, g, t0 = steps[i]
            width = CHUNKS[ch]
            panel, col = divmod(starts[ch], PANEL)
            bank = psum_bank("den")
            for n in range(BANK // width):
                for c, part in enumerate(("x0", "x1")):
                    acc = bank[:, n * width : (n + 1) * width]
                    mx(acc, ("v", PACK * g + t0 + n), c * P, (part, panel), col, width, c == 0, c == 1)
            banks["den", i] = bank

        def num_matmul(i):
            ch, g, t0 = steps[i]
            width = CHUNKS[ch]
            panel, col = divmod(starts[ch], PANEL)
            bank = psum_bank("num")
            for n in range(BANK // width):
                pair, h = divmod(PACK * g + t0 + n, 2)
                mx(bank[:, n * width : (n + 1) * width], ("u", pair), h * P, ("y", panel), col, width, True, True)
            banks["num", i] = bank

        def root(i):
            r = work.tile([P, BANK], F32, name="root")
            nc.scalar.activation(out=r[:], in_=banks["den", i][:], func=ACT.Abs_reciprocal_sqrt)
            roots[i] = r

        def square(i):
            recip = work.tile([P, BANK], F32, name="recip", bufs=RECIP_TILES)
            nc.scalar.activation(out=recip[:], in_=roots[i][:], func=ACT.Square)
            recips[i] = recip

        def divide(i):
            ch, g, t0 = steps[i]
            width = CHUNKS[ch]
            if t0 == 0:
                rows = work.tile([P, PACK * PANEL], BF16, name="ratio_rows", bufs=2)
                ratio_rows[ch, g] = rows[:, 0 : PACK * width].rearrange("p (t n) -> p t n", t=PACK)
            for n in range(BANK // width):
                cols = slice(n * width, (n + 1) * width)
                nc.vector.scalar_tensor_tensor(
                    out=ratio_rows[ch, g][:, t0 + n, :],
                    in0=banks["num", i][:, cols],
                    scalar=bias[:, g, t0 + n : t0 + n + 1],
                    in1=recips[i][:, cols],
                    op0=ALU.add,
                    op1=ALU.mult,
                )

        def stage_ratio(ch, g):
            dst = work.tile([P, PACK * PANEL], BF16, name="ratio_staged", bufs=2, align_bytes=64)
            staged["e", ch, g] = dst
            interleave(nc.vector.tensor_copy, dst, ratio_rows[ch, g], 0, CHUNKS[ch])

        def out_matmul(ch, s0):
            width = CHUNKS[ch]
            bank = psum_bank("aux")
            for n in range(BANK // width):
                for g in range(GROUPS):
                    acc = bank[:, n * width : (n + 1) * width]
                    mx(acc, ("a", s0 + n), g * P, ("e", ch, g), 0, width, g == 0, g == GROUPS - 1)
            banks["out", ch, s0] = bank

        def last_out_pass(s, g):
            width = CHUNKS[last_chunk]
            if g == 0:
                banks["out", last_chunk, s] = psum_bank(("den", "num")[s % 2])
            acc = banks["out", last_chunk, s][:, 0:width]
            mx(acc, ("a", s), g * P, ("e", last_chunk, g), 0, width, g == 0, g == GROUPS - 1)

        def store(ch, s0, count, copy):
            width = CHUNKS[ch]
            result = work.tile([P, BANK], F32, name="result", bufs=RESULT_TILES)
            copy(out=result[:, 0 : count * width], in_=banks["out", ch, s0][:, 0 : count * width])
            nc.sync.dma_start(
                out=out_rows[:, s0 : s0 + count, starts[ch] : starts[ch] + width],
                in_=result[:, 0 : count * width].rearrange("p (s n) -> p s n", s=count),
            )

        phases = ("urgent", "divide", "quantize", "interleave", "hand over", "den", "num", "tensor", "root", "scalar")
        table = {}

        def plan(slot, phase, job, *args):
            table.setdefault((slot, phase), []).append((job, args))

        def plan_weights(key, slot, wait):
            plan(slot, "tensor", turn_weights, key)
            plan(slot + wait, "scalar", stage_weights, key, nc.scalar.copy)
            plan(slot + wait + 1, "quantize" if key[0] == "a" else "urgent", quantize, key, 2 * P)

        def plan_data(key, slot, scalar_cols):
            plan(slot, "interleave", stage_data, key, scalar_cols, False)
            if scalar_cols:
                plan(slot, "scalar", lambda: interleave(nc.scalar.copy, staged[key], data_raw[key], 0, scalar_cols))
            plan(slot + 1, "quantize", quantize, key, PANEL)

        plan_weights(("v", 0), -4, 0)
        plan_data(("x0", 0), -4, HEAD_SHARE)
        plan_data(("x1", 0), -3, HEAD_SHARE)
        plan_weights(("v", 1), -2, 0)
        plan_data(("y", 0), -1, 0)
        plan(-2, "tensor", turn_weights, ("v", 2))
        plan(-1, "interleave", stage_weights, ("v", 2), nc.vector.tensor_copy)
        plan(0, "urgent", quantize, ("v", 2), 2 * P)
        plan_weights(("v", 3), -1, 1)
        for b in range(PACK, 2 * PACK):
            plan_weights(("v", b), b - b % 2 - 3, 1)
        for b in range(2):
            plan_weights(("u", b), b - 1, 1)
            plan_weights(("u", 2 + b), PACK + b, 1)

        late_ratio = ("e", 2, 0)
        pool_tiles = [(part, panel) for panel in (2, 3) for part in ("x0", "y")] + [late_ratio]
        runs = [PACK * (k + 2) + 1 for k in range(len(pool_tiles))]
        in_runs = range(PACK, PACK * (len(runs) + 1))

        for s in range(PACK):
            plan_weights(("a", s), runs[0] + 1 + s, 1)

        plan_data(("x0", 1), 1, 0)
        plan_data(("x1", 1), 3, 0)
        plan(5, "interleave", stage_data, ("y", 1), 0, True)
        plan(runs[0] - 1, "hand over", quantize, ("y", 1), PANEL)
        plan_data(("x1", 2), runs[0] + 1, 0)
        plan_data(("x1", 3), runs[2] + 1, 0)

        def plan_pool_tile(key, slot):
            plan(slot - 1, "hand over", stage_gpsimd, key)
            plan(slot, "interleave",
                 lambda: interleave(nc.vector.tensor_copy, staged[key], source_rows(key), POOL_SHARE, PANEL))
            plan(slot if key == late_ratio else slot + PACK - 1, "hand over", quantize, key, PANEL)

        for key, slot in zip(pool_tiles, runs):
            plan_pool_tile(key, slot)

        for i, (ch, g, t0) in enumerate(steps):
            plan(i - 1, "den", den_matmul, i)
            plan(i, "root", root, i)
            if i in in_runs:
                divide_slot = runs[i // PACK - 1]
                plan(divide_slot - 2 + t0 // 2, "num", num_matmul, i)
            else:
                divide_slot = i + (FIRST_LAG if i < PACK else LAST_LAG)
                plan(i + 1, "num", num_matmul, i)
            plan(divide_slot, "divide", divide, i)
            per_bank = BANK // CHUNKS[ch]
            if t0 + per_bank == PACK:
                if ("e", ch, g) != late_ratio:
                    stage_slot = divide_slot if divide_slot == runs[-1] else divide_slot + 1
                    plan(stage_slot, "interleave", stage_ratio, ch, g)
                    plan(stage_slot + 1, "quantize", quantize, ("e", ch, g), CHUNKS[ch])
                if ch == last_chunk:
                    for s in range(PACK):
                        plan(divide_slot + 2, "tensor", last_out_pass, s, g)
                        if g == GROUPS - 1:
                            copy = (nc.vector.tensor_copy, nc.scalar.copy)[s % 2]
                            plan(divide_slot + 2, "scalar", store, ch, s, 1, copy)
                elif g == GROUPS - 1:
                    first = divide_slot + 1 + OUT_LAGS[ch]
                    for n, s0 in enumerate(range(0, PACK, per_bank)):
                        plan(first + n, "tensor", out_matmul, ch, s0)
                        if (ch, s0) == (1, 0):
                            plan(first + n + 1, "interleave", store, ch, s0, per_bank, nc.vector.tensor_copy)
                        else:
                            plan(first + n + 1, "scalar", store, ch, s0, per_bank, nc.scalar.copy)
        for i in range(len(steps)):
            plan(i + 1, "root", square, i)

        slots = sorted({slot for slot, phase in table})
        for slot in slots:
            for phase in phases:
                for job, args in table.get((slot, phase), []):
                    job(*args)
